import numpy as np
import ml_dtypes


def mxq(x, axis, fmt="e4m3"):
    dtype, down = {"e4m3": (ml_dtypes.float8_e4m3fn, 7), "e5m2": (ml_dtypes.float8_e5m2, 14)}[fmt]
    v = np.moveaxis(np.asarray(x, np.float32).astype(ml_dtypes.bfloat16).astype(np.float64), axis, -1)
    blocks = v.reshape(v.shape[:-1] + (-1, 32))
    amax = np.abs(blocks).max(-1, keepdims=True)
    byte = np.maximum(np.where(amax > 0, np.frexp(amax)[1] - 1 + 127, 0) - down, 1)
    scale = np.exp2(byte - 127.0)
    codes = (blocks / scale).astype(np.float32).astype(dtype).astype(np.float64)
    return np.moveaxis((codes * scale).reshape(v.shape), -1, axis)


WIDE = False


def mx_kscale(k, group=512):
    if not WIDE:
        return np.ones(k)
    levels = np.array([18, -18])
    if group != 512:
        return np.exp2(np.random.permutation(np.resize(levels, k // group))).repeat(group)
    if k % 512:
        return np.exp2(np.random.permutation(np.resize(levels, k // 32))).repeat(32)
    a = np.empty((k // 512, 16))
    for p in range(k // 512):
        a[p, :8] = np.random.permutation(np.resize(levels, 8))
        for g in range(8):
            far = levels[np.abs(levels - a[p, g]) >= 10]
            a[p, g + 8] = far[np.random.randint(len(far))]
    return np.exp2(a.ravel()).repeat(32)


def f64(x):
    return np.asarray(x).astype(np.float64)


def softplus(v):
    return np.log(1.0 + np.exp(v))


def sigmoid(v):
    return 1.0 / (1.0 + np.exp(-v))


G, D, M, N = 4, 128, 128, 512


def setup_inputs():
    n = np.random.standard_normal
    s_d = mx_kscale(D, 0)
    return {
        "x": (n((G, D, N)) * s_d[:, None]).astype(np.float32),
        "w1": (n((G, D, M)) / np.sqrt(D) / s_d[:, None]).astype(np.float32),
        "w2": (n((G, D, M)) / np.sqrt(D) / s_d[:, None]).astype(np.float32),
        "re": (np.random.uniform(50.0, 200.0, (G, M, 1))).astype(np.float32),
        "dx": (n((G, D, N)) * s_d[:, None]).astype(np.float32),
        "og": (np.random.uniform(0.5, 2.0, (G, M, 1))).astype(np.float32),
        "base": (0.3 * n((G, M, N))).astype(np.float32),
    }


def reference(x, w1, w2, re, dx, og, base):
    w1q = mxq(f64(w1), 1, "e4m3")
    xq = mxq(f64(x), 1, "e4m3")
    z1 = w1q.transpose(0, 2, 1) @ xq
    dxq = mxq(f64(dx), 1, "e4m3")
    tz1 = w1q.transpose(0, 2, 1) @ dxq
    w2q = mxq(f64(w2), 1, "e4m3")
    z2 = w2q.transpose(0, 2, 1) @ xq
    tz2 = w2q.transpose(0, 2, 1) @ dxq
    p1 = softplus(z1)
    zs = np.sum(p1, axis=-1, keepdims=True) + f64(re)
    xp1 = tz1 * sigmoid(z1)
    xzs = np.sum(xp1, axis=-1, keepdims=True)
    xh = ((xp1 - xzs * p1 / zs) / zs * np.tanh(z2) + tz2 * (1.0 - np.square(np.tanh(z2))) * p1 / zs) * 512.0
    y = xh * f64(og) + f64(base)
    return y

@@ -1,0 +1,186 @@
+from contextlib import ExitStack
+
+import concourse.mybir as mybir
+
+G, D, M, N = 4, 128, 128, 512
+FLOPS = 4 * 2 * G * D * M * N
+
+F32 = mybir.dt.float32
+BF16 = mybir.dt.bfloat16
+U32 = mybir.dt.uint32
+U8 = mybir.dt.uint8
+FP8X4 = mybir.dt.float8_e4m3fn_x4
+ALU = mybir.AluOpType
+ACT = mybir.ActivationFunctionType
+
+P = 128
+PACK = 4
+ROWS = D // PACK
+TINY = 2.0 ** -60
+X_SPLIT = 344
+
+
+def tile_rows_tnrowshare_kernel(tc, x, w1, w2, re, dx, og, base, out):
+    nc = tc.nc
+    with ExitStack() as ctx:
+        sb = ctx.enter_context(tc.tile_pool(name="sb", bufs=1))
+        ps = ctx.enter_context(tc.psum_pool(name="ps", bufs=1))
+        ctx.enter_context(tc.manual_schedule())
+
+        def load_packed(src, name):
+            width = src.shape[2]
+            raw = sb.tile([P, PACK, width], F32, name=name + "_raw", align_bytes=64)
+            nc.sync.dma_start(out=raw[:], in_=src.rearrange("g (p j) w -> (g p) j w", j=PACK))
+            return raw
+
+        def load_column(src, name):
+            col = sb.tile([P, G, 8], F32, name=name)
+            with nc.allow_non_contiguous_dma(reason="one value a partition"):
+                nc.sync.dma_start(out=col[:, :, 0:1], in_=src.rearrange("g m o -> m g o"))
+            return col
+
+        w1_raw = load_packed(w1, "w1")
+        x_raw = load_packed(x, "x")
+        w2_raw = load_packed(w2, "w2")
+        dx_raw = load_packed(dx, "dx")
+        re_sb = load_column(re, "re_sb")
+        og_sb = load_column(og, "og_sb")
+        base_sb = sb.tile([P, G, N], F32)
+        nc.sync.dma_start(out=base_sb[:], in_=base.rearrange("g m n -> m g n"))
+
+        def word_tile(raw, name):
+            words = sb.tile([P, raw.shape[2], PACK], BF16, name=name + "_bf", align_bytes=64)
+            return words
+
+        def interleave(copy, words, raw, lo, hi):
+            copy(
+                out=words[:, lo:hi, :].rearrange("p (c i) t -> p c t i", i=4),
+                in_=raw[:, :, lo:hi].rearrange("p t (c i) -> p c t i", i=4),
+            )
+
+        def quantize(words, name):
+            width = words.shape[1]
+            codes = sb.tile([P, width], U32, name=name + "_codes", align_bytes=64)
+            scales = sb.tile([P, width], U8, name=name + "_scales", align_bytes=64)
+            nc.vector.quantize_mx(
+                out=codes[:].bitcast(FP8X4), scales=scales[:], in_=words[:].rearrange("p w t -> p (w t)")
+            )
+            return codes, scales
+
+        def product(bank, g, weights, moving):
+            rows = slice(ROWS * g, ROWS * (g + 1))
+            nc.tensor.matmul_mx(
+                out=bank[:],
+                lhsT=weights[0][rows, :].bitcast(FP8X4),
+                lhsT_scale=weights[1][rows, :],
+                rhs=moving[0][rows, :].bitcast(FP8X4),
+                rhs_scale=moving[1][rows, :],
+                start=True,
+                stop=True,
+            )
+
+        bank_a = [ps.tile([M, N], F32, name="bank_a%d" % g) for g in range(G)]
+        bank_b = [ps.tile([M, N], F32, name="bank_b%d" % g) for g in range(G)]
+
+        def planes(name):
+            return [sb.tile([P, N], F32, name="%s%d" % (name, g)) for g in range(G)]
+
+        sneg, th, sq, lns = planes("sneg"), planes("th"), planes("sq"), planes("lns")
+        xn, p1, wn, mm, qq, rr, tt, res = [planes(s) for s in ("xn", "p1", "wn", "mm", "qq", "rr", "tt", "res")]
+        psum1 = [sb.tile([P, 1], F32, name="psum1_%d" % g) for g in range(G)]
+        nzs = [sb.tile([P, 1], F32, name="nzs%d" % g) for g in range(G)]
+        nrz = [sb.tile([P, 1], F32, name="nrz%d" % g) for g in range(G)]
+        pair = sb.tile([P, G, 8], F32)
+        coef = [sb.tile([P, 2], F32, name="coef%d" % g) for g in range(G)]
+
+        tiny = sb.tile([P, 1], F32)
+        nc.vector.memset(tiny[:], TINY)
+        warm = sb.tile([P, 1], F32)
+        nc.scalar.activation(out=warm[:], in_=tiny[:], func=ACT.Sigmoid)
+
+        w1_bf, x_bf, w2_bf, dx_bf = [word_tile(r, s) for r, s in ((w1_raw, "w1"), (x_raw, "x"), (w2_raw, "w2"), (dx_raw, "dx"))]
+        interleave(nc.vector.tensor_copy, w1_bf, w1_raw, 0, M)
+        w1q = quantize(w1_bf, "w1")
+        interleave(nc.vector.tensor_copy, x_bf, x_raw, 0, X_SPLIT)
+        interleave(nc.scalar.copy, x_bf, x_raw, X_SPLIT, N)
+        xq = quantize(x_bf, "x")
+        interleave(nc.scalar.copy, w2_bf, w2_raw, 0, M)
+        w2q = quantize(w2_bf, "w2")
+        for g in range(G):
+            product(bank_a[g], g, w1q, xq)
+        for g in range(G):
+            product(bank_b[g], g, w2q, xq)
+        interleave(nc.vector.tensor_copy, dx_bf, dx_raw, 0, N)
+        dxq = quantize(dx_bf, "dx")
+
+        for g in range(G):
+            nc.scalar.activation(out=th[g][:], in_=bank_b[g][:], func=ACT.Tanh)
+            nc.scalar.activation(out=sneg[g][:], in_=bank_a[g][:], func=ACT.Sigmoid, scale=-1.0)
+        for g in range(G):
+            product(bank_b[g], g, w1q, dxq)
+        nc.scalar.activation(out=pair[:, :, 1:2], in_=og_sb[:, :, 0:1], func=ACT.Copy, scale=float(N))
+        for g in range(G):
+            nc.vector.scalar_tensor_tensor(
+                out=xn[g][:], in0=sneg[g][:], scalar=1.0, in1=bank_b[g][:],
+                op0=ALU.subtract, op1=ALU.mult, accum_out=pair[:, g, 0:1],
+            )
+            product(bank_b[g], g, w2q, dxq)
+        for g in range(G):
+            nc.scalar.activation(out=lns[g][:], in_=sneg[g][:], func=ACT.Ln, bias=tiny[:])
+            nc.scalar.activation(out=sq[g][:], in_=th[g][:], func=ACT.Square)
+
+        def do_m(g):
+            nc.vector.tensor_tensor(out=mm[g][:], in0=xn[g][:], in1=th[g][:], op=ALU.mult)
+
+        def do_p1(g):
+            nc.vector.scalar_tensor_tensor(
+                out=p1[g][:], in0=lns[g][:], scalar=-1.0, in1=bank_a[g][:],
+                op0=ALU.mult, op1=ALU.max, accum_out=psum1[g][:],
+            )
+
+        def do_w(g):
+            nc.vector.scalar_tensor_tensor(
+                out=wn[g][:], in0=sq[g][:], scalar=1.0, in1=bank_b[g][:], op0=ALU.subtract, op1=ALU.mult
+            )
+
+        def do_add(g):
+            nc.vector.tensor_scalar(
+                out=nzs[g][:], in0=psum1[g][:], scalar1=re_sb[:, g, 0:1], scalar2=-1.0, op0=ALU.add, op1=ALU.mult
+            )
+
+        def do_rec(g):
+            nc.vector.reciprocal(out=nrz[g][:], in_=nzs[g][:])
+
+        def do_mul(g):
+            nc.vector.tensor_scalar(
+                out=coef[g][:], in0=pair[:, g, 0:2], scalar1=nrz[g][:], scalar2=None, op0=ALU.mult
+            )
+
+        def do_q(g):
+            nc.vector.scalar_tensor_tensor(
+                out=qq[g][:], in0=th[g][:], scalar=coef[g][:, 0:1], in1=wn[g][:], op0=ALU.mult, op1=ALU.add
+            )
+
+        def do_r(g):
+            nc.vector.tensor_tensor(out=rr[g][:], in0=qq[g][:], in1=p1[g][:], op=ALU.mult)
+
+        def do_t(g):
+            nc.vector.scalar_tensor_tensor(
+                out=tt[g][:], in0=mm[g][:], scalar=coef[g][:, 1:2], in1=base_sb[:, g, :], op0=ALU.mult, op1=ALU.add
+            )
+
+        def do_out(g):
+            nc.vector.scalar_tensor_tensor(
+                out=res[g][:], in0=rr[g][:], scalar=coef[g][:, 1:2], in1=tt[g][:], op0=ALU.mult, op1=ALU.add
+            )
+            nc.sync.dma_start(out=out[g], in_=res[g][:])
+
+        steps = [
+            (do_m, 0), (do_m, 1), (do_m, 2), (do_p1, 0), (do_w, 0), (do_add, 0), (do_m, 3), (do_rec, 0),
+            (do_p1, 1), (do_mul, 0), (do_w, 1), (do_add, 1), (do_q, 0), (do_rec, 1), (do_t, 0), (do_mul, 1),
+            (do_r, 0), (do_p1, 2), (do_out, 0), (do_add, 2), (do_q, 1), (do_rec, 2), (do_t, 1), (do_mul, 2),
+            (do_r, 1), (do_p1, 3), (do_out, 1), (do_add, 3), (do_w, 2), (do_rec, 3), (do_w, 3), (do_mul, 3),
+            (do_q, 2), (do_t, 2), (do_r, 2), (do_q, 3), (do_out, 2), (do_r, 3), (do_t, 3), (do_out, 3),
+        ]
+        for fn, g in steps:
+            fn(g)

@@ -39,8 +39,8 @@ def tile_rows_tnrowshare_kernel(tc, x, w1, w2, re, dx, og, base, out):
                 nc.sync.dma_start(out=col[:, :, 0:1], in_=src.rearrange("g m o -> m g o"))
             return col
 
-        w1_raw = load_packed(w1, "w1")
         x_raw = load_packed(x, "x")
+        w1_raw = load_packed(w1, "w1")
         w2_raw = load_packed(w2, "w2")
         dx_raw = load_packed(dx, "dx")
         re_sb = load_column(re, "re_sb")
@@ -99,11 +99,11 @@ def tile_rows_tnrowshare_kernel(tc, x, w1, w2, re, dx, og, base, out):
         nc.scalar.activation(out=warm[:], in_=tiny[:], func=ACT.Sigmoid)
 
         w1_bf, x_bf, w2_bf, dx_bf = [word_tile(r, s) for r, s in ((w1_raw, "w1"), (x_raw, "x"), (w2_raw, "w2"), (dx_raw, "dx"))]
-        interleave(nc.vector.tensor_copy, w1_bf, w1_raw, 0, M)
-        w1q = quantize(w1_bf, "w1")
         interleave(nc.vector.tensor_copy, x_bf, x_raw, 0, X_SPLIT)
         interleave(nc.scalar.copy, x_bf, x_raw, X_SPLIT, N)
+        interleave(nc.scalar.copy, w1_bf, w1_raw, 0, M)
         xq = quantize(x_bf, "x")
+        w1q = quantize(w1_bf, "w1")
         interleave(nc.scalar.copy, w2_bf, w2_raw, 0, M)
         w2q = quantize(w2_bf, "w2")
         for g in range(G):
@@ -114,23 +114,27 @@ def tile_rows_tnrowshare_kernel(tc, x, w1, w2, re, dx, og, base, out):
         dxq = quantize(dx_bf, "dx")
 
         for g in range(G):
-            nc.scalar.activation(out=th[g][:], in_=bank_b[g][:], func=ACT.Tanh)
             nc.scalar.activation(out=sneg[g][:], in_=bank_a[g][:], func=ACT.Sigmoid, scale=-1.0)
         for g in range(G):
+            nc.scalar.activation(out=th[g][:], in_=bank_b[g][:], func=ACT.Tanh, scale=-1.0)
+        for g in range(G):
             product(bank_b[g], g, w1q, dxq)
-        nc.scalar.activation(out=pair[:, :, 1:2], in_=og_sb[:, :, 0:1], func=ACT.Copy, scale=float(N))
         for g in range(G):
             nc.vector.scalar_tensor_tensor(
                 out=xn[g][:], in0=sneg[g][:], scalar=1.0, in1=bank_b[g][:],
                 op0=ALU.subtract, op1=ALU.mult, accum_out=pair[:, g, 0:1],
             )
             product(bank_b[g], g, w2q, dxq)
-        for g in range(G):
+            nc.gpsimd.tensor_tensor(out=mm[g][:], in0=xn[g][:], in1=th[g][:], op=ALU.mult)
+
+        def do_ln(g):
             nc.scalar.activation(out=lns[g][:], in_=sneg[g][:], func=ACT.Ln, bias=tiny[:])
+
+        def do_sq(g):
             nc.scalar.activation(out=sq[g][:], in_=th[g][:], func=ACT.Square)
 
-        def do_m(g):
-            nc.vector.tensor_tensor(out=mm[g][:], in0=xn[g][:], in1=th[g][:], op=ALU.mult)
+        def do_og(g):
+            nc.scalar.activation(out=pair[:, :, 1:2], in_=og_sb[:, :, 0:1], func=ACT.Copy, scale=-float(N))
 
         def do_p1(g):
             nc.vector.scalar_tensor_tensor(
@@ -144,17 +148,13 @@ def tile_rows_tnrowshare_kernel(tc, x, w1, w2, re, dx, og, base, out):
             )
 
         def do_add(g):
-            nc.vector.tensor_scalar(
-                out=nzs[g][:], in0=psum1[g][:], scalar1=re_sb[:, g, 0:1], scalar2=-1.0, op0=ALU.add, op1=ALU.mult
-            )
+            nc.scalar.activation(out=nzs[g][:], in_=psum1[g][:], func=ACT.Identity, bias=re_sb[:, g, 0:1])
 
         def do_rec(g):
             nc.vector.reciprocal(out=nrz[g][:], in_=nzs[g][:])
 
         def do_mul(g):
-            nc.vector.tensor_scalar(
-                out=coef[g][:], in0=pair[:, g, 0:2], scalar1=nrz[g][:], scalar2=None, op0=ALU.mult
-            )
+            nc.scalar.activation(out=coef[g][:], in_=pair[:, g, 0:2], func=ACT.Copy, scale=nrz[g][:])
 
         def do_q(g):
             nc.vector.scalar_tensor_tensor(
@@ -162,25 +162,30 @@ def tile_rows_tnrowshare_kernel(tc, x, w1, w2, re, dx, og, base, out):
             )
 
         def do_r(g):
-            nc.vector.tensor_tensor(out=rr[g][:], in0=qq[g][:], in1=p1[g][:], op=ALU.mult)
+            eng = nc.gpsimd if g < 2 else nc.vector
+            eng.tensor_tensor(out=rr[g][:], in0=qq[g][:], in1=p1[g][:], op=ALU.mult)
 
         def do_t(g):
             nc.vector.scalar_tensor_tensor(
-                out=tt[g][:], in0=mm[g][:], scalar=coef[g][:, 1:2], in1=base_sb[:, g, :], op0=ALU.mult, op1=ALU.add
+                out=tt[g][:], in0=mm[g][:], scalar=coef[g][:, 1:2], in1=base_sb[:, g, :], op0=ALU.mult, op1=ALU.subtract
             )
 
         def do_out(g):
-            nc.vector.scalar_tensor_tensor(
-                out=res[g][:], in0=rr[g][:], scalar=coef[g][:, 1:2], in1=tt[g][:], op0=ALU.mult, op1=ALU.add
-            )
-            nc.sync.dma_start(out=out[g], in_=res[g][:])
+            pieces = 2 if g == G - 1 else 1
+            for h in range(pieces):
+                cols = slice(h * N // pieces, (h + 1) * N // pieces)
+                nc.vector.scalar_tensor_tensor(
+                    out=res[g][:, cols], in0=rr[g][:, cols], scalar=coef[g][:, 1:2], in1=tt[g][:, cols],
+                    op0=ALU.mult, op1=ALU.subtract,
+                )
+                nc.sync.dma_start(out=out[g, :, cols], in_=res[g][:, cols])
 
         steps = [
-            (do_m, 0), (do_m, 1), (do_m, 2), (do_p1, 0), (do_w, 0), (do_add, 0), (do_m, 3), (do_rec, 0),
-            (do_p1, 1), (do_mul, 0), (do_w, 1), (do_add, 1), (do_q, 0), (do_rec, 1), (do_t, 0), (do_mul, 1),
-            (do_r, 0), (do_p1, 2), (do_out, 0), (do_add, 2), (do_q, 1), (do_rec, 2), (do_t, 1), (do_mul, 2),
-            (do_r, 1), (do_p1, 3), (do_out, 1), (do_add, 3), (do_w, 2), (do_rec, 3), (do_w, 3), (do_mul, 3),
-            (do_q, 2), (do_t, 2), (do_r, 2), (do_q, 3), (do_out, 2), (do_r, 3), (do_t, 3), (do_out, 3),
+            (do_ln, 0), (do_sq, 0), (do_p1, 0), (do_w, 0), (do_ln, 1), (do_add, 0), (do_sq, 1), (do_p1, 1), (do_rec, 0),
+            (do_w, 1), (do_add, 1), (do_og, 0), (do_mul, 0), (do_ln, 2), (do_rec, 1), (do_mul, 1), (do_q, 0), (do_r, 0),
+            (do_sq, 2), (do_p1, 2), (do_w, 2), (do_ln, 3), (do_add, 2), (do_sq, 3), (do_rec, 2), (do_mul, 2), (do_q, 1), (do_r, 1),
+            (do_p1, 3), (do_w, 3), (do_add, 3), (do_t, 0), (do_rec, 3), (do_mul, 3), (do_q, 2), (do_out, 0), (do_t, 1),
+            (do_r, 2), (do_out, 1), (do_q, 3), (do_t, 2), (do_r, 3), (do_out, 2), (do_t, 3), (do_out, 3),
         ]
         for fn, g in steps:
             fn(g)

@@ -33,28 +33,37 @@ def tile_rows_tnrowshare_kernel(tc, x, w1, w2, re, dx, og, base, out):
             nc.sync.dma_start(out=raw[:], in_=src.rearrange("g (p j) w -> (g p) j w", j=PACK))
             return raw
 
+        def load_halves(src, name):
+            rows = src.rearrange("g (p j) w -> (g p) j w", j=PACK)
+            halves = []
+            for h in range(2):
+                raw = sb.tile([P, 2, N], F32, name="%s_raw%d" % (name, h), align_bytes=64)
+                nc.sync.dma_start(out=raw[:], in_=rows[:, 2 * h : 2 * h + 2, :])
+                halves.append(raw)
+            return halves
+
         def load_column(src, name):
             col = sb.tile([P, G, 8], F32, name=name)
             with nc.allow_non_contiguous_dma(reason="one value a partition"):
                 nc.sync.dma_start(out=col[:, :, 0:1], in_=src.rearrange("g m o -> m g o"))
             return col
 
-        x_raw = load_packed(x, "x")
-        w1_raw = load_packed(w1, "w1")
+        x_raw = load_halves(x, "x")
         w2_raw = load_packed(w2, "w2")
-        dx_raw = load_packed(dx, "dx")
+        w1_raw = load_packed(w1, "w1")
+        dx_raw = load_halves(dx, "dx")
         re_sb = load_column(re, "re_sb")
         og_sb = load_column(og, "og_sb")
         base_sb = sb.tile([P, G, N], F32)
         nc.sync.dma_start(out=base_sb[:], in_=base.rearrange("g m n -> m g n"))
 
-        def word_tile(raw, name):
-            words = sb.tile([P, raw.shape[2], PACK], BF16, name=name + "_bf", align_bytes=64)
+        def word_tile(width, name):
+            words = sb.tile([P, width, PACK], BF16, name=name + "_bf", align_bytes=64)
             return words
 
-        def interleave(copy, words, raw, lo, hi):
+        def interleave(copy, words, raw, lo, hi, first=0):
             copy(
-                out=words[:, lo:hi, :].rearrange("p (c i) t -> p c t i", i=4),
+                out=words[:, lo:hi, first : first + raw.shape[1]].rearrange("p (c i) t -> p c t i", i=4),
                 in_=raw[:, :, lo:hi].rearrange("p t (c i) -> p c t i", i=4),
             )
 
@@ -98,34 +107,43 @@ def tile_rows_tnrowshare_kernel(tc, x, w1, w2, re, dx, og, base, out):
         warm = sb.tile([P, 1], F32)
         nc.scalar.activation(out=warm[:], in_=tiny[:], func=ACT.Sigmoid)
 
-        w1_bf, x_bf, w2_bf, dx_bf = [word_tile(r, s) for r, s in ((w1_raw, "w1"), (x_raw, "x"), (w2_raw, "w2"), (dx_raw, "dx"))]
-        interleave(nc.vector.tensor_copy, x_bf, x_raw, 0, X_SPLIT)
-        interleave(nc.scalar.copy, x_bf, x_raw, X_SPLIT, N)
-        interleave(nc.scalar.copy, w1_bf, w1_raw, 0, M)
-        xq = quantize(x_bf, "x")
-        w1q = quantize(w1_bf, "w1")
+        w1_bf, x_bf, w2_bf, dx_bf = [word_tile(r, s) for r, s in ((M, "w1"), (N, "x"), (M, "w2"), (N, "dx"))]
+        interleave(nc.vector.tensor_copy, x_bf, x_raw[0], 0, N)
+        interleave(nc.vector.tensor_copy, x_bf, x_raw[1], 0, X_SPLIT, 2)
+        interleave(nc.scalar.copy, x_bf, x_raw[1], X_SPLIT, N, 2)
         interleave(nc.scalar.copy, w2_bf, w2_raw, 0, M)
+        xq = quantize(x_bf, "x")
         w2q = quantize(w2_bf, "w2")
-        for g in range(G):
-            product(bank_a[g], g, w1q, xq)
+        interleave(nc.scalar.copy, w1_bf, w1_raw, 0, M)
+        w1q = quantize(w1_bf, "w1")
         for g in range(G):
             product(bank_b[g], g, w2q, xq)
-        interleave(nc.vector.tensor_copy, dx_bf, dx_raw, 0, N)
+        for g in range(G):
+            product(bank_a[g], g, w1q, xq)
+        interleave(nc.vector.tensor_copy, dx_bf, dx_raw[0], 0, N)
+        interleave(nc.vector.tensor_copy, dx_bf, dx_raw[1], 0, N, 2)
         dxq = quantize(dx_bf, "dx")
 
         for g in range(G):
-            nc.scalar.activation(out=sneg[g][:], in_=bank_a[g][:], func=ACT.Sigmoid, scale=-1.0)
-        for g in range(G):
             nc.scalar.activation(out=th[g][:], in_=bank_b[g][:], func=ACT.Tanh, scale=-1.0)
         for g in range(G):
+            nc.scalar.activation(out=sneg[g][:], in_=bank_a[g][:], func=ACT.Sigmoid, scale=-1.0)
+        for g in range(G):
             product(bank_b[g], g, w1q, dxq)
+        mm = [mm[0]] + xn[: G - 1]
+
+        def do_m(g):
+            eng = nc.gpsimd if g in (0, G - 1) else nc.vector
+            eng.tensor_tensor(out=mm[g][:], in0=xn[g][:], in1=th[g][:], op=ALU.mult)
+
         for g in range(G):
             nc.vector.scalar_tensor_tensor(
                 out=xn[g][:], in0=sneg[g][:], scalar=1.0, in1=bank_b[g][:],
                 op0=ALU.subtract, op1=ALU.mult, accum_out=pair[:, g, 0:1],
             )
             product(bank_b[g], g, w2q, dxq)
-            nc.gpsimd.tensor_tensor(out=mm[g][:], in0=xn[g][:], in1=th[g][:], op=ALU.mult)
+        for g in range(G):
+            do_m(g)
 
         def do_ln(g):
             nc.scalar.activation(out=lns[g][:], in_=sneg[g][:], func=ACT.Ln, bias=tiny[:])
@@ -163,7 +181,10 @@ def tile_rows_tnrowshare_kernel(tc, x, w1, w2, re, dx, og, base, out):
 
         def do_r(g):
             eng = nc.gpsimd if g < 2 else nc.vector
-            eng.tensor_tensor(out=rr[g][:], in0=qq[g][:], in1=p1[g][:], op=ALU.mult)
+            pieces = 2 if g == G - 1 else 1
+            for h in range(pieces):
+                cols = slice(h * N // pieces, (h + 1) * N // pieces)
+                eng.tensor_tensor(out=rr[g][:, cols], in0=qq[g][:, cols], in1=p1[g][:, cols], op=ALU.mult)
 
         def do_t(g):
             nc.vector.scalar_tensor_tensor(
@@ -180,12 +201,6 @@ def tile_rows_tnrowshare_kernel(tc, x, w1, w2, re, dx, og, base, out):
                 )
                 nc.sync.dma_start(out=out[g, :, cols], in_=res[g][:, cols])
 
-        steps = [
-            (do_ln, 0), (do_sq, 0), (do_p1, 0), (do_w, 0), (do_ln, 1), (do_add, 0), (do_sq, 1), (do_p1, 1), (do_rec, 0),
-            (do_w, 1), (do_add, 1), (do_og, 0), (do_mul, 0), (do_ln, 2), (do_rec, 1), (do_mul, 1), (do_q, 0), (do_r, 0),
-            (do_sq, 2), (do_p1, 2), (do_w, 2), (do_ln, 3), (do_add, 2), (do_sq, 3), (do_rec, 2), (do_mul, 2), (do_q, 1), (do_r, 1),
-            (do_p1, 3), (do_w, 3), (do_add, 3), (do_t, 0), (do_rec, 3), (do_mul, 3), (do_q, 2), (do_out, 0), (do_t, 1),
-            (do_r, 2), (do_out, 1), (do_q, 3), (do_t, 2), (do_r, 3), (do_out, 2), (do_t, 3), (do_out, 3),
-        ]
+        steps = [(do_ln, 0), (do_sq, 0), (do_p1, 0), (do_w, 0), (do_ln, 1), (do_add, 0), (do_rec, 0), (do_og, 0), (do_sq, 1), (do_p1, 1), (do_mul, 0), (do_ln, 2), (do_add, 1), (do_q, 0), (do_r, 0), (do_w, 1), (do_rec, 1), (do_sq, 2), (do_mul, 1), (do_p1, 2), (do_ln, 3), (do_add, 2), (do_q, 1), (do_r, 1), (do_sq, 3), (do_w, 2), (do_rec, 2), (do_mul, 2), (do_p1, 3), (do_w, 3), (do_add, 3), (do_t, 0), (do_rec, 3), (do_mul, 3), (do_q, 2), (do_out, 0), (do_t, 1), (do_r, 2), (do_out, 1), (do_t, 2), (do_t, 3), (do_q, 3), (do_out, 2), (do_r, 3), (do_out, 3)]
         for fn, g in steps:
             fn(g)

@@ -16,8 +16,16 @@ ACT = mybir.ActivationFunctionType
 P = 128
 PACK = 4
 ROWS = D // PACK
-TINY = 2.0 ** -60
-X_SPLIT = 344
+HALF = N // 2
+LAST = G - 1
+PAD = 8
+RUN = 4
+
+LOG_FLOOR_AT = 36.0
+
+X_SPLIT = 368
+
+POOL_SHARED = 2
 
 
 def tile_rows_tnrowshare_kernel(tc, x, w1, w2, re, dx, og, base, out):
@@ -28,53 +36,51 @@ def tile_rows_tnrowshare_kernel(tc, x, w1, w2, re, dx, og, base, out):
         ctx.enter_context(tc.manual_schedule())
 
         def load_packed(src, name):
-            width = src.shape[2]
-            raw = sb.tile([P, PACK, width], F32, name=name + "_raw", align_bytes=64)
-            nc.sync.dma_start(out=raw[:], in_=src.rearrange("g (p j) w -> (g p) j w", j=PACK))
+            raw = sb.tile([P, PACK, src.shape[2]], F32, name=name + "_raw", align_bytes=64)
+            nc.sync.dma_start(out=raw[:], in_=src.rearrange("g (p t) w -> (g p) t w", t=PACK))
             return raw
 
-        def load_halves(src, name):
-            rows = src.rearrange("g (p j) w -> (g p) j w", j=PACK)
-            halves = []
-            for h in range(2):
-                raw = sb.tile([P, 2, N], F32, name="%s_raw%d" % (name, h), align_bytes=64)
-                nc.sync.dma_start(out=raw[:], in_=rows[:, 2 * h : 2 * h + 2, :])
-                halves.append(raw)
-            return halves
+        def load_row_values(src, name):
+            values = sb.tile([P, G, PAD], F32, name=name)
+            with nc.allow_non_contiguous_dma(reason="one value a partition and group"):
+                nc.sync.dma_start(out=values[:, :, 0:1], in_=src.rearrange("g m o -> m g o"))
+            return values
 
-        def load_column(src, name):
-            col = sb.tile([P, G, 8], F32, name=name)
-            with nc.allow_non_contiguous_dma(reason="one value a partition"):
-                nc.sync.dma_start(out=col[:, :, 0:1], in_=src.rearrange("g m o -> m g o"))
-            return col
-
-        x_raw = load_halves(x, "x")
+        x_raw = load_packed(x, "x")
         w2_raw = load_packed(w2, "w2")
         w1_raw = load_packed(w1, "w1")
-        dx_raw = load_halves(dx, "dx")
-        re_sb = load_column(re, "re_sb")
-        og_sb = load_column(og, "og_sb")
+        dx_raw = load_packed(dx, "dx")
+        re_sb = load_row_values(re, "re_sb")
+        og_sb = load_row_values(og, "og_sb")
         base_sb = sb.tile([P, G, N], F32)
         nc.sync.dma_start(out=base_sb[:], in_=base.rearrange("g m n -> m g n"))
 
-        def word_tile(width, name):
-            words = sb.tile([P, width, PACK], BF16, name=name + "_bf", align_bytes=64)
-            return words
+        floor_at = sb.tile([P, 1], F32)
+        nc.vector.memset(floor_at[:], LOG_FLOOR_AT)
+        floor = sb.tile([P, 1], F32)
+        nc.scalar.activation(out=floor[:], in_=floor_at[:], func=ACT.Sigmoid, scale=-1.0)
 
-        def interleave(copy, words, raw, lo, hi, first=0):
-            copy(
-                out=words[:, lo:hi, first : first + raw.shape[1]].rearrange("p (c i) t -> p c t i", i=4),
-                in_=raw[:, :, lo:hi].rearrange("p t (c i) -> p c t i", i=4),
-            )
+        def rounded_tile(width, name):
+            return sb.tile([P, width, PACK], BF16, name=name + "_bf", align_bytes=64)
 
-        def quantize(words, name):
-            width = words.shape[1]
+        def operand(width, name):
             codes = sb.tile([P, width], U32, name=name + "_codes", align_bytes=64)
             scales = sb.tile([P, width], U8, name=name + "_scales", align_bytes=64)
-            nc.vector.quantize_mx(
-                out=codes[:].bitcast(FP8X4), scales=scales[:], in_=words[:].rearrange("p w t -> p (w t)")
-            )
             return codes, scales
+
+        def interleave(copy, rounded, first, raw, lo, hi):
+            copy(
+                out=rounded[:, lo - first : hi - first, :].rearrange("p (c i) t -> p c t i", i=RUN),
+                in_=raw[:, :, lo:hi].rearrange("p t (c i) -> p c t i", i=RUN),
+            )
+
+        def quantize(dst, first, rounded):
+            cols = slice(first, first + rounded.shape[1])
+            nc.vector.quantize_mx(
+                out=dst[0][:, cols].bitcast(FP8X4),
+                scales=dst[1][:, cols],
+                in_=rounded[:].rearrange("p w t -> p (w t)"),
+            )
 
         def product(bank, g, weights, moving):
             rows = slice(ROWS * g, ROWS * (g + 1))
@@ -88,119 +94,144 @@ def tile_rows_tnrowshare_kernel(tc, x, w1, w2, re, dx, og, base, out):
                 stop=True,
             )
 
-        bank_a = [ps.tile([M, N], F32, name="bank_a%d" % g) for g in range(G)]
-        bank_b = [ps.tile([M, N], F32, name="bank_b%d" % g) for g in range(G)]
+        z1_bank = [ps.tile([M, N], F32, name="z1_bank%d" % g) for g in range(G)]
+        turn_bank = [ps.tile([M, N], F32, name="turn_bank%d" % g) for g in range(G)]
 
-        def planes(name):
-            return [sb.tile([P, N], F32, name="%s%d" % (name, g)) for g in range(G)]
+        w1_bf, w2_bf = rounded_tile(M, "w1"), rounded_tile(M, "w2")
+        x_bf = [rounded_tile(HALF, "x%d" % h) for h in range(2)]
+        dx_bf = [rounded_tile(HALF, "dx%d" % h) for h in range(2)]
+        w1q, w2q, xq, dxq = operand(M, "w1"), operand(M, "w2"), operand(N, "x"), operand(N, "dx")
 
-        sneg, th, sq, lns = planes("sneg"), planes("th"), planes("sq"), planes("lns")
-        xn, p1, wn, mm, qq, rr, tt, res = [planes(s) for s in ("xn", "p1", "wn", "mm", "qq", "rr", "tt", "res")]
-        psum1 = [sb.tile([P, 1], F32, name="psum1_%d" % g) for g in range(G)]
-        nzs = [sb.tile([P, 1], F32, name="nzs%d" % g) for g in range(G)]
-        nrz = [sb.tile([P, 1], F32, name="nrz%d" % g) for g in range(G)]
-        pair = sb.tile([P, G, 8], F32)
-        coef = [sb.tile([P, 2], F32, name="coef%d" % g) for g in range(G)]
-
-        tiny = sb.tile([P, 1], F32)
-        nc.vector.memset(tiny[:], TINY)
-        warm = sb.tile([P, 1], F32)
-        nc.scalar.activation(out=warm[:], in_=tiny[:], func=ACT.Sigmoid)
-
-        w1_bf, x_bf, w2_bf, dx_bf = [word_tile(r, s) for r, s in ((M, "w1"), (N, "x"), (M, "w2"), (N, "dx"))]
-        interleave(nc.vector.tensor_copy, x_bf, x_raw[0], 0, N)
-        interleave(nc.vector.tensor_copy, x_bf, x_raw[1], 0, X_SPLIT, 2)
-        interleave(nc.scalar.copy, x_bf, x_raw[1], X_SPLIT, N, 2)
-        interleave(nc.scalar.copy, w2_bf, w2_raw, 0, M)
-        xq = quantize(x_bf, "x")
-        w2q = quantize(w2_bf, "w2")
-        interleave(nc.scalar.copy, w1_bf, w1_raw, 0, M)
-        w1q = quantize(w1_bf, "w1")
+        interleave(nc.vector.tensor_copy, x_bf[0], 0, x_raw, 0, HALF)
+        interleave(nc.vector.tensor_copy, x_bf[1], HALF, x_raw, HALF, X_SPLIT)
+        interleave(nc.scalar.copy, x_bf[1], HALF, x_raw, X_SPLIT, N)
+        interleave(nc.scalar.copy, w2_bf, 0, w2_raw, 0, M)
+        for h in range(2):
+            quantize(xq, h * HALF, x_bf[h])
+        quantize(w2q, 0, w2_bf)
+        interleave(nc.scalar.copy, w1_bf, 0, w1_raw, 0, M)
+        quantize(w1q, 0, w1_bf)
         for g in range(G):
-            product(bank_b[g], g, w2q, xq)
+            product(turn_bank[g], g, w2q, xq)
         for g in range(G):
-            product(bank_a[g], g, w1q, xq)
-        interleave(nc.vector.tensor_copy, dx_bf, dx_raw[0], 0, N)
-        interleave(nc.vector.tensor_copy, dx_bf, dx_raw[1], 0, N, 2)
-        dxq = quantize(dx_bf, "dx")
+            product(z1_bank[g], g, w1q, xq)
+        for h in range(2):
+            interleave(nc.vector.tensor_copy, dx_bf[h], h * HALF, dx_raw, h * HALF, (h + 1) * HALF)
+        for h in range(2):
+            quantize(dxq, h * HALF, dx_bf[h])
+
+        def group_tiles(name, width):
+            return [sb.tile([P, width], F32, name="%s%d" % (name, g)) for g in range(G)]
+
+        sig_neg, tanh_neg, tanh_sq, log_sig, xp_neg, p1, slope, mixed, shared, partial, result = [
+            group_tiles(name, N)
+            for name in ("sig_neg", "tanh_neg", "tanh_sq", "log_sig", "xp_neg", "p1", "slope", "mixed", "shared", "partial", "result")
+        ]
+        p1_sum, zs, inv_zs = group_tiles("p1_sum", 1), group_tiles("zs", 1), group_tiles("inv_zs", 1)
+        numer = sb.tile([P, G, PAD], F32)
+        coef = group_tiles("coef", 2)
 
         for g in range(G):
-            nc.scalar.activation(out=th[g][:], in_=bank_b[g][:], func=ACT.Tanh, scale=-1.0)
+            nc.scalar.activation(out=tanh_neg[g][:], in_=turn_bank[g][:], func=ACT.Tanh, scale=-1.0)
         for g in range(G):
-            nc.scalar.activation(out=sneg[g][:], in_=bank_a[g][:], func=ACT.Sigmoid, scale=-1.0)
+            nc.scalar.activation(out=sig_neg[g][:], in_=z1_bank[g][:], func=ACT.Sigmoid, scale=-1.0)
         for g in range(G):
-            product(bank_b[g], g, w1q, dxq)
-        mm = [mm[0]] + xn[: G - 1]
-
-        def do_m(g):
-            eng = nc.gpsimd if g in (0, G - 1) else nc.vector
-            eng.tensor_tensor(out=mm[g][:], in0=xn[g][:], in1=th[g][:], op=ALU.mult)
-
+            product(turn_bank[g], g, w1q, dxq)
         for g in range(G):
             nc.vector.scalar_tensor_tensor(
-                out=xn[g][:], in0=sneg[g][:], scalar=1.0, in1=bank_b[g][:],
-                op0=ALU.subtract, op1=ALU.mult, accum_out=pair[:, g, 0:1],
+                out=xp_neg[g][:], in0=sig_neg[g][:], scalar=1.0, in1=turn_bank[g][:],
+                op0=ALU.subtract, op1=ALU.mult, accum_out=numer[:, g, 0:1],
             )
-            product(bank_b[g], g, w2q, dxq)
+            product(turn_bank[g], g, w2q, dxq)
+
+        cross_first = sb.tile([P, N], F32)
+        cross = [cross_first] + xp_neg[:LAST]
         for g in range(G):
-            do_m(g)
+            engine = nc.gpsimd if g in (0, LAST) else nc.vector
+            engine.tensor_tensor(out=cross[g][:], in0=xp_neg[g][:], in1=tanh_neg[g][:], op=ALU.mult)
 
-        def do_ln(g):
-            nc.scalar.activation(out=lns[g][:], in_=sneg[g][:], func=ACT.Ln, bias=tiny[:])
+        def make_log(g):
+            nc.scalar.activation(out=log_sig[g][:], in_=sig_neg[g][:], func=ACT.Ln, bias=floor[:])
 
-        def do_sq(g):
-            nc.scalar.activation(out=sq[g][:], in_=th[g][:], func=ACT.Square)
+        def make_square(g):
+            nc.scalar.activation(out=tanh_sq[g][:], in_=tanh_neg[g][:], func=ACT.Square)
 
-        def do_og(g):
-            nc.scalar.activation(out=pair[:, :, 1:2], in_=og_sb[:, :, 0:1], func=ACT.Copy, scale=-float(N))
+        def make_zs(g):
+            nc.scalar.activation(out=zs[g][:], in_=p1_sum[g][:], func=ACT.Identity, bias=re_sb[:, g, 0:1])
 
-        def do_p1(g):
+        def make_inverse(g):
+            nc.vector.reciprocal(out=inv_zs[g][:], in_=zs[g][:])
+
+        def make_coef(g):
+            nc.scalar.activation(out=coef[g][:], in_=numer[:, g, 0:2], func=ACT.Copy, scale=inv_zs[g][:])
+
+        def make_p1(g):
             nc.vector.scalar_tensor_tensor(
-                out=p1[g][:], in0=lns[g][:], scalar=-1.0, in1=bank_a[g][:],
-                op0=ALU.mult, op1=ALU.max, accum_out=psum1[g][:],
+                out=p1[g][:], in0=log_sig[g][:], scalar=-1.0, in1=z1_bank[g][:],
+                op0=ALU.mult, op1=ALU.max, accum_out=p1_sum[g][:],
             )
 
-        def do_w(g):
+        def make_slope(g):
             nc.vector.scalar_tensor_tensor(
-                out=wn[g][:], in0=sq[g][:], scalar=1.0, in1=bank_b[g][:], op0=ALU.subtract, op1=ALU.mult
+                out=slope[g][:], in0=tanh_sq[g][:], scalar=1.0, in1=turn_bank[g][:],
+                op0=ALU.subtract, op1=ALU.mult,
             )
 
-        def do_add(g):
-            nc.scalar.activation(out=nzs[g][:], in_=psum1[g][:], func=ACT.Identity, bias=re_sb[:, g, 0:1])
-
-        def do_rec(g):
-            nc.vector.reciprocal(out=nrz[g][:], in_=nzs[g][:])
-
-        def do_mul(g):
-            nc.scalar.activation(out=coef[g][:], in_=pair[:, g, 0:2], func=ACT.Copy, scale=nrz[g][:])
-
-        def do_q(g):
+        def make_mixed(g):
             nc.vector.scalar_tensor_tensor(
-                out=qq[g][:], in0=th[g][:], scalar=coef[g][:, 0:1], in1=wn[g][:], op0=ALU.mult, op1=ALU.add
+                out=mixed[g][:], in0=tanh_neg[g][:], scalar=coef[g][:, 0:1], in1=slope[g][:],
+                op0=ALU.mult, op1=ALU.add,
             )
 
-        def do_r(g):
-            eng = nc.gpsimd if g < 2 else nc.vector
-            pieces = 2 if g == G - 1 else 1
-            for h in range(pieces):
-                cols = slice(h * N // pieces, (h + 1) * N // pieces)
-                eng.tensor_tensor(out=rr[g][:, cols], in0=qq[g][:, cols], in1=p1[g][:, cols], op=ALU.mult)
+        def make_shared(g, engine):
+            engine.tensor_tensor(out=shared[g][:], in0=mixed[g][:], in1=p1[g][:], op=ALU.mult)
 
-        def do_t(g):
+        def make_partial(g, cols):
             nc.vector.scalar_tensor_tensor(
-                out=tt[g][:], in0=mm[g][:], scalar=coef[g][:, 1:2], in1=base_sb[:, g, :], op0=ALU.mult, op1=ALU.subtract
+                out=partial[g][:, cols], in0=cross[g][:, cols], scalar=coef[g][:, 1:2], in1=base_sb[:, g, cols],
+                op0=ALU.mult, op1=ALU.subtract,
             )
 
-        def do_out(g):
-            pieces = 2 if g == G - 1 else 1
-            for h in range(pieces):
-                cols = slice(h * N // pieces, (h + 1) * N // pieces)
-                nc.vector.scalar_tensor_tensor(
-                    out=res[g][:, cols], in0=rr[g][:, cols], scalar=coef[g][:, 1:2], in1=tt[g][:, cols],
-                    op0=ALU.mult, op1=ALU.subtract,
-                )
-                nc.sync.dma_start(out=out[g, :, cols], in_=res[g][:, cols])
+        def finish(g, cols):
+            nc.vector.scalar_tensor_tensor(
+                out=result[g][:, cols], in0=shared[g][:, cols], scalar=coef[g][:, 1:2], in1=partial[g][:, cols],
+                op0=ALU.mult, op1=ALU.subtract,
+            )
+            nc.sync.dma_start(out=out[g, :, cols], in_=result[g][:, cols])
 
-        steps = [(do_ln, 0), (do_sq, 0), (do_p1, 0), (do_w, 0), (do_ln, 1), (do_add, 0), (do_rec, 0), (do_og, 0), (do_sq, 1), (do_p1, 1), (do_mul, 0), (do_ln, 2), (do_add, 1), (do_q, 0), (do_r, 0), (do_w, 1), (do_rec, 1), (do_sq, 2), (do_mul, 1), (do_p1, 2), (do_ln, 3), (do_add, 2), (do_q, 1), (do_r, 1), (do_sq, 3), (do_w, 2), (do_rec, 2), (do_mul, 2), (do_p1, 3), (do_w, 3), (do_add, 3), (do_t, 0), (do_rec, 3), (do_mul, 3), (do_q, 2), (do_out, 0), (do_t, 1), (do_r, 2), (do_out, 1), (do_t, 2), (do_t, 3), (do_q, 3), (do_out, 2), (do_r, 3), (do_out, 3)]
-        for fn, g in steps:
-            fn(g)
+        whole = slice(0, N)
+        halves = [slice(0, HALF), slice(HALF, N)]
+
+        make_log(0)
+        make_square(0)
+        nc.scalar.activation(out=numer[:, :, 1:2], in_=og_sb[:, :, 0:1], func=ACT.Copy, scale=-float(N))
+        make_p1(0)
+        make_slope(0)
+        for g in range(LAST):
+            make_log(g + 1)
+            make_zs(g)
+            make_square(g + 1)
+            make_inverse(g)
+            make_coef(g)
+            if g > 0:
+                make_slope(g)
+            make_p1(g + 1)
+            if g < POOL_SHARED:
+                make_mixed(g)
+                make_shared(g, nc.gpsimd)
+        make_slope(LAST)
+        make_zs(LAST)
+
+        make_partial(0, whole)
+        make_inverse(LAST)
+        make_coef(LAST)
+        for g in range(POOL_SHARED, G):
+            make_mixed(g)
+            finish(g - POOL_SHARED, whole)
+            make_partial(g - 1, whole)
+            make_shared(g, nc.vector)
+        finish(LAST - 1, whole)
+        for cols in halves:
+            make_partial(LAST, cols)
+        for cols in halves:
+            finish(LAST, cols)

from contextlib import ExitStack

import concourse.mybir as mybir

G, D, M, N = 4, 128, 128, 512
FLOPS = 4 * 2 * G * D * M * N

F32 = mybir.dt.float32
BF16 = mybir.dt.bfloat16
U32 = mybir.dt.uint32
U8 = mybir.dt.uint8
FP8X4 = mybir.dt.float8_e4m3fn_x4
ALU = mybir.AluOpType
ACT = mybir.ActivationFunctionType

P = 128
PACK = 4
ROWS = D // PACK
HALF = N // 2
LAST = G - 1
PAD = 8
RUN = 4

LOG_FLOOR_AT = 36.0

X_SPLIT = 368

POOL_SHARED = 2


def tile_rows_tnrowshare_kernel(tc, x, w1, w2, re, dx, og, base, out):
    nc = tc.nc
    with ExitStack() as ctx:
        sb = ctx.enter_context(tc.tile_pool(name="sb", bufs=1))
        ps = ctx.enter_context(tc.psum_pool(name="ps", bufs=1))
        ctx.enter_context(tc.manual_schedule())

        def load_packed(src, name):
            raw = sb.tile([P, PACK, src.shape[2]], F32, name=name + "_raw", align_bytes=64)
            nc.sync.dma_start(out=raw[:], in_=src.rearrange("g (p t) w -> (g p) t w", t=PACK))
            return raw

        def load_row_values(src, name):
            values = sb.tile([P, G, PAD], F32, name=name)
            with nc.allow_non_contiguous_dma(reason="one value a partition and group"):
                nc.sync.dma_start(out=values[:, :, 0:1], in_=src.rearrange("g m o -> m g o"))
            return values

        x_raw = load_packed(x, "x")
        w2_raw = load_packed(w2, "w2")
        w1_raw = load_packed(w1, "w1")
        dx_raw = load_packed(dx, "dx")
        re_sb = load_row_values(re, "re_sb")
        og_sb = load_row_values(og, "og_sb")
        base_sb = sb.tile([P, G, N], F32)
        nc.sync.dma_start(out=base_sb[:], in_=base.rearrange("g m n -> m g n"))

        floor_at = sb.tile([P, 1], F32)
        nc.vector.memset(floor_at[:], LOG_FLOOR_AT)
        floor = sb.tile([P, 1], F32)
        nc.scalar.activation(out=floor[:], in_=floor_at[:], func=ACT.Sigmoid, scale=-1.0)

        def rounded_tile(width, name):
            return sb.tile([P, width, PACK], BF16, name=name + "_bf", align_bytes=64)

        def operand(width, name):
            codes = sb.tile([P, width], U32, name=name + "_codes", align_bytes=64)
            scales = sb.tile([P, width], U8, name=name + "_scales", align_bytes=64)
            return codes, scales

        def interleave(copy, rounded, first, raw, lo, hi):
            copy(
                out=rounded[:, lo - first : hi - first, :].rearrange("p (c i) t -> p c t i", i=RUN),
                in_=raw[:, :, lo:hi].rearrange("p t (c i) -> p c t i", i=RUN),
            )

        def quantize(dst, first, rounded):
            cols = slice(first, first + rounded.shape[1])
            nc.vector.quantize_mx(
                out=dst[0][:, cols].bitcast(FP8X4),
                scales=dst[1][:, cols],
                in_=rounded[:].rearrange("p w t -> p (w t)"),
            )

        def product(bank, g, weights, moving):
            rows = slice(ROWS * g, ROWS * (g + 1))
            nc.tensor.matmul_mx(
                out=bank[:],
                lhsT=weights[0][rows, :].bitcast(FP8X4),
                lhsT_scale=weights[1][rows, :],
                rhs=moving[0][rows, :].bitcast(FP8X4),
                rhs_scale=moving[1][rows, :],
                start=True,
                stop=True,
            )

        z1_bank = [ps.tile([M, N], F32, name="z1_bank%d" % g) for g in range(G)]
        turn_bank = [ps.tile([M, N], F32, name="turn_bank%d" % g) for g in range(G)]

        w1_bf, w2_bf = rounded_tile(M, "w1"), rounded_tile(M, "w2")
        x_bf = [rounded_tile(HALF, "x%d" % h) for h in range(2)]
        dx_bf = [rounded_tile(HALF, "dx%d" % h) for h in range(2)]
        w1q, w2q, xq, dxq = operand(M, "w1"), operand(M, "w2"), operand(N, "x"), operand(N, "dx")

        interleave(nc.vector.tensor_copy, x_bf[0], 0, x_raw, 0, HALF)
        interleave(nc.vector.tensor_copy, x_bf[1], HALF, x_raw, HALF, X_SPLIT)
        interleave(nc.scalar.copy, x_bf[1], HALF, x_raw, X_SPLIT, N)
        interleave(nc.scalar.copy, w2_bf, 0, w2_raw, 0, M)
        for h in range(2):
            quantize(xq, h * HALF, x_bf[h])
        quantize(w2q, 0, w2_bf)
        interleave(nc.scalar.copy, w1_bf, 0, w1_raw, 0, M)
        quantize(w1q, 0, w1_bf)
        for g in range(G):
            product(turn_bank[g], g, w2q, xq)
        for g in range(G):
            product(z1_bank[g], g, w1q, xq)
        for h in range(2):
            interleave(nc.vector.tensor_copy, dx_bf[h], h * HALF, dx_raw, h * HALF, (h + 1) * HALF)
        for h in range(2):
            quantize(dxq, h * HALF, dx_bf[h])

        def group_tiles(name, width):
            return [sb.tile([P, width], F32, name="%s%d" % (name, g)) for g in range(G)]

        sig_neg, tanh_neg, tanh_sq, log_sig, xp_neg, p1, slope, mixed, shared, partial, result = [
            group_tiles(name, N)
            for name in ("sig_neg", "tanh_neg", "tanh_sq", "log_sig", "xp_neg", "p1", "slope", "mixed", "shared", "partial", "result")
        ]
        p1_sum, zs, inv_zs = group_tiles("p1_sum", 1), group_tiles("zs", 1), group_tiles("inv_zs", 1)
        numer = sb.tile([P, G, PAD], F32)
        coef = group_tiles("coef", 2)

        for g in range(G):
            nc.scalar.activation(out=tanh_neg[g][:], in_=turn_bank[g][:], func=ACT.Tanh, scale=-1.0)
        for g in range(G):
            nc.scalar.activation(out=sig_neg[g][:], in_=z1_bank[g][:], func=ACT.Sigmoid, scale=-1.0)
        for g in range(G):
            product(turn_bank[g], g, w1q, dxq)
        for g in range(G):
            nc.vector.scalar_tensor_tensor(
                out=xp_neg[g][:], in0=sig_neg[g][:], scalar=1.0, in1=turn_bank[g][:],
                op0=ALU.subtract, op1=ALU.mult, accum_out=numer[:, g, 0:1],
            )
            product(turn_bank[g], g, w2q, dxq)

        cross_first = sb.tile([P, N], F32)
        cross = [cross_first] + xp_neg[:LAST]
        for g in range(G):
            engine = nc.gpsimd if g in (0, LAST) else nc.vector
            engine.tensor_tensor(out=cross[g][:], in0=xp_neg[g][:], in1=tanh_neg[g][:], op=ALU.mult)

        def make_log(g):
            nc.scalar.activation(out=log_sig[g][:], in_=sig_neg[g][:], func=ACT.Ln, bias=floor[:])

        def make_square(g):
            nc.scalar.activation(out=tanh_sq[g][:], in_=tanh_neg[g][:], func=ACT.Square)

        def make_zs(g):
            nc.scalar.activation(out=zs[g][:], in_=p1_sum[g][:], func=ACT.Identity, bias=re_sb[:, g, 0:1])

        def make_inverse(g):
            nc.vector.reciprocal(out=inv_zs[g][:], in_=zs[g][:])

        def make_coef(g):
            nc.scalar.activation(out=coef[g][:], in_=numer[:, g, 0:2], func=ACT.Copy, scale=inv_zs[g][:])

        def make_p1(g):
            nc.vector.scalar_tensor_tensor(
                out=p1[g][:], in0=log_sig[g][:], scalar=-1.0, in1=z1_bank[g][:],
                op0=ALU.mult, op1=ALU.max, accum_out=p1_sum[g][:],
            )

        def make_slope(g):
            nc.vector.scalar_tensor_tensor(
                out=slope[g][:], in0=tanh_sq[g][:], scalar=1.0, in1=turn_bank[g][:],
                op0=ALU.subtract, op1=ALU.mult,
            )

        def make_mixed(g):
            nc.vector.scalar_tensor_tensor(
                out=mixed[g][:], in0=tanh_neg[g][:], scalar=coef[g][:, 0:1], in1=slope[g][:],
                op0=ALU.mult, op1=ALU.add,
            )

        def make_shared(g, engine):
            engine.tensor_tensor(out=shared[g][:], in0=mixed[g][:], in1=p1[g][:], op=ALU.mult)

        def make_partial(g, cols):
            nc.vector.scalar_tensor_tensor(
                out=partial[g][:, cols], in0=cross[g][:, cols], scalar=coef[g][:, 1:2], in1=base_sb[:, g, cols],
                op0=ALU.mult, op1=ALU.subtract,
            )

        def finish(g, cols):
            nc.vector.scalar_tensor_tensor(
                out=result[g][:, cols], in0=shared[g][:, cols], scalar=coef[g][:, 1:2], in1=partial[g][:, cols],
                op0=ALU.mult, op1=ALU.subtract,
            )
            nc.sync.dma_start(out=out[g, :, cols], in_=result[g][:, cols])

        whole = slice(0, N)
        halves = [slice(0, HALF), slice(HALF, N)]

        make_log(0)
        make_square(0)
        nc.scalar.activation(out=numer[:, :, 1:2], in_=og_sb[:, :, 0:1], func=ACT.Copy, scale=-float(N))
        make_p1(0)
        make_slope(0)
        for g in range(LAST):
            make_log(g + 1)
            make_zs(g)
            make_square(g + 1)
            make_inverse(g)
            make_coef(g)
            if g > 0:
                make_slope(g)
            make_p1(g + 1)
            if g < POOL_SHARED:
                make_mixed(g)
                make_shared(g, nc.gpsimd)
        make_slope(LAST)
        make_zs(LAST)

        make_partial(0, whole)
        make_inverse(LAST)
        make_coef(LAST)
        for g in range(POOL_SHARED, G):
            make_mixed(g)
            finish(g - POOL_SHARED, whole)
            make_partial(g - 1, whole)
            make_shared(g, nc.vector)
        finish(LAST - 1, whole)
        for cols in halves:
            make_partial(LAST, cols)
        for cols in halves:
            finish(LAST, cols)
